import numpy as np
import ml_dtypes


def mxq(x, axis, fmt="e4m3"):
    dtype, down = {"e4m3": (ml_dtypes.float8_e4m3fn, 7), "e5m2": (ml_dtypes.float8_e5m2, 14)}[fmt]
    v = np.moveaxis(np.asarray(x, np.float32).astype(ml_dtypes.bfloat16).astype(np.float64), axis, -1)
    blocks = v.reshape(v.shape[:-1] + (-1, 32))
    amax = np.abs(blocks).max(-1, keepdims=True)
    byte = np.maximum(np.where(amax > 0, np.frexp(amax)[1] - 1 + 127, 0) - down, 1)
    scale = np.exp2(byte - 127.0)
    codes = (blocks / scale).astype(np.float32).astype(dtype).astype(np.float64)
    return np.moveaxis((codes * scale).reshape(v.shape), -1, axis)


WIDE = False


def mx_kscale(k):
    if not WIDE:
        return np.ones(k)
    levels = np.array([30, -30])
    if k % 512:
        return np.exp2(np.random.permutation(np.resize(levels, k // 32))).repeat(32)
    a = np.empty((k // 512, 16))
    for p in range(k // 512):
        a[p, :8] = np.random.permutation(np.resize(levels, 8))
        for g in range(8):
            far = levels[np.abs(levels - a[p, g]) >= 10]
            a[p, g + 8] = far[np.random.randint(len(far))]
    return np.exp2(a.ravel()).repeat(32)


def f64(x):
    return np.asarray(x).astype(np.float64)


def striped(idx):
    return np.tile(np.asarray(idx).reshape(-1, 16).T, (8, 1)).astype(np.uint16)


def unstriped(offs):
    return offs[:16].T.reshape(-1).astype(np.int64)


def striped8(idx):
    return np.asarray(idx).reshape(8, -1, 16).transpose(0, 2, 1).reshape(128, -1).astype(np.uint16)


def unstriped8(offs):
    return offs.reshape(8, 16, -1).transpose(0, 2, 1).reshape(8, -1).astype(np.int64)


def pick8(x, idx, run):
    r = np.arange(len(x))
    return x[r[:, None], idx[r % (8 * run) // run]]


E2M1 = np.array([0.0, 0.5, 1.0, 1.5, 2.0, 3.0, 4.0, 6.0, -0.0, -0.5, -1.0, -1.5, -2.0, -3.0, -4.0, -6.0])


def pack_weight(w, fmt):
    k, n = w.shape
    w = f64(np.asarray(w, np.float32).astype(ml_dtypes.bfloat16)).reshape(k // 32, 32, n)
    amax = np.abs(w).max(1)
    if fmt in ("e4m3", "e5m2"):
        byte = np.frexp(amax)[1] - 1 + 127 - (7 if fmt == "e4m3" else 14)
    else:
        mant, ex = np.frexp(amax / 6.0)
        byte = np.where(mant > 0.5, ex, ex - 1) + 127
    byte = np.clip(np.where(amax > 0, byte, 1), 1, 254)
    scaled = (w * np.exp2(127.0 - byte)[:, None, :]).reshape(k, n).astype(np.float32)
    by_word = np.ascontiguousarray(scaled.reshape(k // 512, 128, 4, n).transpose(0, 1, 3, 2))
    if fmt in ("e4m3", "e5m2"):
        words = by_word.astype(ml_dtypes.float8_e4m3fn if fmt == "e4m3" else ml_dtypes.float8_e5m2).view(np.uint8)
    else:
        c = by_word.astype(ml_dtypes.float4_e2m1fn).view(np.uint8) & 0xF
        words = (c[..., 0::2] | (c[..., 1::2] << 4)).reshape(k // 512, 128, 2 * n)
    return np.ascontiguousarray(words), np.ascontiguousarray(byte.astype(np.uint8).reshape(k // 512, 16, n))


def unpack_weight(words, scales, fmt):
    g, _, n = scales.shape
    words = np.ascontiguousarray(words).reshape(g, 128, n, -1)
    if fmt in ("e4m3", "e5m2"):
        vals = words.view(ml_dtypes.float8_e4m3fn if fmt == "e4m3" else ml_dtypes.float8_e5m2).astype(np.float64)
    else:
        nib = np.empty((g, 128, n, 4), np.uint8)
        nib[..., 0::2] = words & 0xF
        nib[..., 1::2] = words >> 4
        vals = E2M1[nib]
    vals = vals * np.repeat(np.exp2(scales.astype(np.float64) - 127.0), 8, axis=1)[..., None]
    return vals.transpose(0, 1, 3, 2).reshape(g * 512, n)


K, T, J, R, O, N = 512, 1024, 256, 512, 128, 256


def setup_inputs():
    n = np.random.standard_normal
    idx = np.random.permutation(T)[:J]
    idx2 = np.stack([np.random.permutation(J)[:O] for _ in range(8)])
    idx3 = np.random.permutation(T)[:O]
    fk = mx_kscale(K)
    fr = mx_kscale(R)
    xtp = pack_weight(n((K, T)) / fk[:, None], "e4m3")
    wp = pack_weight(n((K, R)) * 1 / np.sqrt(K) * fk[:, None] * fr, "e2m1")
    wbp = pack_weight(n((R, N)) * 1 / np.sqrt(R) / fr[:, None], "e5m2")
    wsp = pack_weight(n((K, N)) * 1 / np.sqrt(K) * fk[:, None], "e5m2")
    return {
        "xt_words": xtp[0],
        "xt_scales": xtp[1],
        "w_words": wp[0],
        "w_scales": wp[1],
        "sa": (np.random.uniform(0.5, 1.6, (R, 1))).astype(np.float32),
        "wb_words": wbp[0],
        "wb_scales": wbp[1],
        "ws_words": wsp[0],
        "ws_scales": wsp[1],
        "offs": striped(idx),
        "offs2": striped8(idx2),
        "offs3": striped(idx3),
    }


def reference(xt_words, xt_scales, w_words, w_scales, sa, wb_words, wb_scales, ws_words, ws_scales, offs, offs2, offs3):
    idx = unstriped(offs)
    idx2 = unstriped8(offs2)
    idx3 = unstriped(offs3)
    xtu = unpack_weight(xt_words, xt_scales, "e4m3")
    wu = unpack_weight(w_words, w_scales, "e2m1")
    wbu = unpack_weight(wb_words, wb_scales, "e5m2")
    wsu = unpack_weight(ws_words, ws_scales, "e5m2")
    xtidxg = xtu[:, idx]
    a = wu.T @ xtidxg
    g1 = np.maximum(a, 0.0)
    hid = pick8(g1, idx2, 64) * f64(sa)
    hidq = mxq(hid, 0, "e4m3")
    xtidx3g = xtu[:, idx3]
    y = wbu.T @ hidq + wsu.T @ xtidx3g
    return y

@@ -1,0 +1,175 @@
+from contextlib import ExitStack
+
+import concourse.mybir as mybir
+
+K, T, J, R, O, N = 512, 1024, 256, 512, 128, 256
+FLOPS = 2 * K * R * J + 2 * R * N * O + 2 * K * N * O
+
+F32 = mybir.dt.float32
+BF16 = mybir.dt.bfloat16
+I32 = mybir.dt.int32
+U32 = mybir.dt.uint32
+U16 = mybir.dt.uint16
+U8 = mybir.dt.uint8
+E4M3 = mybir.dt.float8_e4m3fn_x4
+E5M2 = mybir.dt.float8_e5m2_x4
+E2M1 = mybir.dt.float4_e2m1fn_x4
+COPY = mybir.ActivationFunctionType.Copy
+RELU = mybir.ActivationFunctionType.Relu
+
+P = 128
+PACK = 4
+QUADS = 4
+
+
+def tile_list_groupshift_solo_further_plain_kernel(
+    tc, xt_words, xt_scales, w_words, w_scales, sa, wb_words, wb_scales, ws_words, ws_scales, offs, offs2, offs3, out
+):
+    nc = tc.nc
+
+    def words(ap):
+        return ap[0].rearrange("p n t -> p (n t)").bitcast(I32)
+
+    with ExitStack() as ctx:
+        sb = ctx.enter_context(tc.tile_pool(name="sb", bufs=1))
+        ps = ctx.enter_context(tc.psum_pool(name="ps", bufs=1))
+
+        list1 = sb.tile([P, J // 16], U16, name="list1")
+        list2 = sb.tile([P, O // 16], U16, name="list2")
+        list3 = sb.tile([P, O // 16], U16, name="list3")
+        x_words = sb.tile([P, T], U32, name="x_words", align_bytes=64)
+        x_plane = sb.tile([P, T], U8, name="x_plane", align_bytes=64)
+        w_raw = sb.tile([P, 2 * R], U8, name="w_raw", align_bytes=64)
+        w_two = sb.tile([P, 2, R], U8, name="w_two", align_bytes=64)
+        sa_t = sb.tile([P, PACK], F32, name="sa_t")
+        ws_w = sb.tile([P, N], U32, name="ws_w", align_bytes=64)
+        wb_w = sb.tile([P, N], U32, name="wb_w", align_bytes=64)
+        w_stage = sb.tile([4, QUADS, R // 4], I32, name="w_stage")
+        out_two = sb.tile([P, 2, 2, N], U8, name="out_two", align_bytes=64)
+        ws_plane = out_two[:, 0, 0, :]
+        wb_plane = out_two[:, 0, 1, :]
+
+        nc.vector.memset(w_two[0:64].bitcast(I32), 0)
+        nc.vector.memset(x_plane[:].bitcast(I32), 0)
+        nc.vector.memset(out_two[0:64].bitcast(I32), 0)
+
+        nc.sync.dma_start(list1[:], offs)
+        nc.scalar.dma_start(w_stage[:], w_scales[0].bitcast(I32).rearrange("(q r) n -> r q n", r=4))
+        nc.sync.dma_start(x_words[:].bitcast(I32), words(xt_words))
+        nc.sync.dma_start(w_raw[:].bitcast(I32), w_words[0].bitcast(I32))
+        for q in range(QUADS):
+            queue = nc.scalar if q < 2 else nc.sync
+            queue.dma_start(
+                x_plane[32 * q : 32 * q + 4, :].bitcast(I32), xt_scales[0, 4 * q : 4 * q + 4, :].bitcast(I32)
+            )
+        nc.sync.dma_start(list3[:], offs3)
+        nc.sync.dma_start(list2[:], offs2)
+        nc.sync.dma_start(sa_t[:], sa.rearrange("(p t) o -> p (t o)", t=PACK))
+        nc.sync.dma_start(ws_w[:].bitcast(I32), words(ws_words))
+        nc.sync.dma_start(wb_w[:].bitcast(I32), words(wb_words))
+        for i, scales in enumerate((ws_scales, wb_scales)):
+            rows = scales[0].bitcast(I32).rearrange("(a b r) n -> b r a n", a=2, b=2)
+            for b in range(2):
+                nc.sync.dma_start(out_two[32 * b : 32 * b + 4, :, i, :].bitcast(I32), rows[b])
+
+        H = J // 2
+        by_parity = w_stage[:].rearrange("r (a b) n -> r b a n", b=2)
+        nc.vector.tensor_copy(w_two[32:36].bitcast(I32), by_parity[:, 1])
+        nc.scalar.copy(w_two[0:4].bitcast(U32), by_parity[:, 0].bitcast(U32))
+        xg_plane = sb.tile([P, J], U8, name="xg_plane", align_bytes=64)
+        nc.vector.tensor_copy(xg_plane[:], x_plane[:].indirect(list1[:]))
+        nc.vector.tensor_copy(w_two[64:128, 0, :].bitcast(I32), w_two[0:64, 1, :].bitcast(I32))
+
+        wp_words = sb.tile([P, PACK, 2 * P], U8, name="wp_words", align_bytes=64)
+        w16 = w_raw[:].bitcast(U16).rearrange("p (m t) -> p t m", t=PACK)
+        for t in range(PACK):
+            nc.scalar.copy(wp_words[:, t, :].bitcast(U16), w16[:, t, :])
+
+        wp_plane = sb.tile([P, PACK, P], U8, name="wp_plane", align_bytes=64)
+        w8 = w_two[:, 0, :].rearrange("p (m t) -> p t m", t=PACK)
+        xg_words = [sb.tile([P, H], U32, name="xg_words%d" % u, align_bytes=64) for u in range(2)]
+        for u in range(2):
+            nc.vector.tensor_copy(xg_words[u][:], x_words[:].indirect(list1[:, 8 * u : 8 * u + 8]))
+            nc.vector.tensor_copy(wp_plane[:, 2 * u : 2 * u + 2, :], w8[:, 2 * u : 2 * u + 2, :])
+        x3_words = sb.tile([P, O], U32, name="x3_words", align_bytes=64)
+        nc.vector.tensor_copy(x3_words[:], x_words[:].indirect(list3[:]))
+
+        hid = sb.tile([P, PACK, O], BF16, name="hid", align_bytes=64)
+        g1 = [sb.tile([P, J], F32, name="g1_%d" % t, align_bytes=64) for t in range(PACK)]
+        split = [[ps.tile([P, H], F32, name="a%d_%d" % (t, u)) for u in range(2)] for t in range(2)]
+        whole = [ps.tile([P, J], F32, name="a%d" % t) for t in range(2, PACK)]
+
+        def first(t, u):
+            dst = split[t][u][:] if t < 2 else whole[t - 2][:, u * H : (u + 1) * H]
+            nc.tensor.matmul_mx(
+                out=dst,
+                lhsT=wp_words[:, t, :].bitcast(E2M1),
+                lhsT_scale=wp_plane[:, t, :],
+                rhs=xg_words[u][:].bitcast(E4M3),
+                rhs_scale=xg_plane[:, u * H : (u + 1) * H],
+                start=True,
+                stop=True,
+            )
+
+        def pick(t):
+            nc.scalar.activation(hid[:, t, :], g1[t][:].indirect(list2[:]), COPY, scale=sa_t[:, t : t + 1])
+
+        for t in range(2):
+            first(t, 0)
+            nc.scalar.activation(g1[t][:, 0:H], split[t][0][:], RELU)
+        for t in range(2):
+            first(t, 1)
+            nc.vector.tensor_scalar_max(g1[t][:, H:J], split[t][1][:], 0.0)
+            pick(t)
+        for t in range(2, PACK):
+            first(t, 0)
+            first(t, 1)
+            nc.vector.tensor_scalar_max(g1[t][:], whole[t - 2][:], 0.0)
+            pick(t)
+
+        x3_plane = sb.tile([P, O], U8, name="x3_plane", align_bytes=64)
+        nc.vector.tensor_copy(x3_plane[:], x_plane[:].indirect(list3[:]))
+
+        nc.vector.tensor_copy(out_two[64:128, 0].bitcast(I32), out_two[0:64, 1].bitcast(I32))
+
+        ys = [ps.tile([P, O], F32, name="y%d" % h) for h in range(2)]
+        for h in range(2):
+            cols = slice(h * P, (h + 1) * P)
+            nc.tensor.matmul_mx(
+                out=ys[h][:],
+                lhsT=ws_w[:, cols].bitcast(E5M2),
+                lhsT_scale=ws_plane[:, cols],
+                rhs=x3_words[:].bitcast(E4M3),
+                rhs_scale=x3_plane[:],
+                start=True,
+                stop=False,
+            )
+
+        woven = sb.tile([P, O, PACK], BF16, name="woven", align_bytes=64)
+        nc.vector.tensor_copy(
+            woven[:].rearrange("p (c i) t -> p c t i", i=4),
+            hid[:].rearrange("p t (c i) -> p c t i", i=4),
+        )
+        h_words = sb.tile([P, O], U32, name="h_words", align_bytes=64)
+        h_plane = sb.tile([P, O], U8, name="h_plane", align_bytes=64)
+        nc.vector.quantize_mx(
+            out=h_words[:].bitcast(E4M3), scales=h_plane[:], in_=woven[:].rearrange("p o t -> p (o t)")
+        )
+
+        for h in range(2):
+            cols = slice(h * P, (h + 1) * P)
+            nc.tensor.matmul_mx(
+                out=ys[h][:],
+                lhsT=wb_w[:, cols].bitcast(E5M2),
+                lhsT_scale=wb_plane[:, cols],
+                rhs=h_words[:].bitcast(E4M3),
+                rhs_scale=h_plane[:],
+                start=False,
+                stop=True,
+            )
+        res0 = sb.tile([P, O], F32, name="res0")
+        res1 = sb.tile([P, O], F32, name="res1")
+        nc.vector.tensor_copy(res0[:], ys[0][:])
+        nc.sync.dma_start(out[0:P, :], res0[:])
+        nc.scalar.copy(res1[:], ys[1][:])
+        nc.scalar.dma_start(out[P : 2 * P, :], res1[:])

@@ -45,92 +45,72 @@ def tile_list_groupshift_solo_further_plain_kernel(
         ws_w = sb.tile([P, N], U32, name="ws_w", align_bytes=64)
         wb_w = sb.tile([P, N], U32, name="wb_w", align_bytes=64)
         w_stage = sb.tile([4, QUADS, R // 4], I32, name="w_stage")
-        out_two = sb.tile([P, 2, 2, N], U8, name="out_two", align_bytes=64)
-        ws_plane = out_two[:, 0, 0, :]
-        wb_plane = out_two[:, 0, 1, :]
+        ws_plane = sb.tile([P, N], U8, name="ws_plane", align_bytes=64)
+        wb_plane = sb.tile([P, N], U8, name="wb_plane", align_bytes=64)
 
-        nc.vector.memset(w_two[0:64].bitcast(I32), 0)
+        def load_plane(plane, scales):
+            for q in range(QUADS):
+                nc.sync.dma_start(
+                    plane[32 * q : 32 * q + 4, :].bitcast(I32), scales[0, 4 * q : 4 * q + 4, :].bitcast(I32)
+                )
+
         nc.vector.memset(x_plane[:].bitcast(I32), 0)
-        nc.vector.memset(out_two[0:64].bitcast(I32), 0)
+        nc.vector.memset(w_two[0:64].bitcast(I32), 0)
+        nc.vector.memset(ws_plane[:].bitcast(I32), 0)
+        nc.vector.memset(wb_plane[:].bitcast(I32), 0)
 
         nc.sync.dma_start(list1[:], offs)
         nc.scalar.dma_start(w_stage[:], w_scales[0].bitcast(I32).rearrange("(q r) n -> r q n", r=4))
-        nc.sync.dma_start(x_words[:].bitcast(I32), words(xt_words))
+        nc.scalar.dma_start(x_words[:].bitcast(I32), words(xt_words))
         nc.sync.dma_start(w_raw[:].bitcast(I32), w_words[0].bitcast(I32))
-        for q in range(QUADS):
-            queue = nc.scalar if q < 2 else nc.sync
-            queue.dma_start(
-                x_plane[32 * q : 32 * q + 4, :].bitcast(I32), xt_scales[0, 4 * q : 4 * q + 4, :].bitcast(I32)
-            )
+        load_plane(x_plane, xt_scales)
+        nc.gpsimd.dma_start(sa_t[:], sa.rearrange("(p t) o -> p (t o)", t=PACK))
         nc.sync.dma_start(list3[:], offs3)
         nc.sync.dma_start(list2[:], offs2)
-        nc.sync.dma_start(sa_t[:], sa.rearrange("(p t) o -> p (t o)", t=PACK))
-        nc.sync.dma_start(ws_w[:].bitcast(I32), words(ws_words))
-        nc.sync.dma_start(wb_w[:].bitcast(I32), words(wb_words))
-        for i, scales in enumerate((ws_scales, wb_scales)):
-            rows = scales[0].bitcast(I32).rearrange("(a b r) n -> b r a n", a=2, b=2)
-            for b in range(2):
-                nc.sync.dma_start(out_two[32 * b : 32 * b + 4, :, i, :].bitcast(I32), rows[b])
+        nc.gpsimd.dma_start(ws_w[:].bitcast(I32), words(ws_words))
+        nc.gpsimd.dma_start(wb_w[:].bitcast(I32), words(wb_words))
+        load_plane(ws_plane, ws_scales)
+        load_plane(wb_plane, wb_scales)
 
-        H = J // 2
         by_parity = w_stage[:].rearrange("r (a b) n -> r b a n", b=2)
-        nc.vector.tensor_copy(w_two[32:36].bitcast(I32), by_parity[:, 1])
-        nc.scalar.copy(w_two[0:4].bitcast(U32), by_parity[:, 0].bitcast(U32))
+        for b in range(2):
+            nc.vector.tensor_copy(w_two[32 * b : 32 * b + 4].bitcast(I32), by_parity[:, b])
+        nc.vector.tensor_copy(w_two[64:128, 0, :].bitcast(I32), w_two[0:64, 1, :].bitcast(I32))
         xg_plane = sb.tile([P, J], U8, name="xg_plane", align_bytes=64)
         nc.vector.tensor_copy(xg_plane[:], x_plane[:].indirect(list1[:]))
-        nc.vector.tensor_copy(w_two[64:128, 0, :].bitcast(I32), w_two[0:64, 1, :].bitcast(I32))
+        wp_plane = sb.tile([P, PACK, P], U8, name="wp_plane", align_bytes=64)
+        nc.vector.tensor_copy(wp_plane[:], w_two[:, 0, :].rearrange("p (m t) -> p t m", t=PACK))
 
         wp_words = sb.tile([P, PACK, 2 * P], U8, name="wp_words", align_bytes=64)
         w16 = w_raw[:].bitcast(U16).rearrange("p (m t) -> p t m", t=PACK)
         for t in range(PACK):
             nc.scalar.copy(wp_words[:, t, :].bitcast(U16), w16[:, t, :])
 
-        wp_plane = sb.tile([P, PACK, P], U8, name="wp_plane", align_bytes=64)
-        w8 = w_two[:, 0, :].rearrange("p (m t) -> p t m", t=PACK)
-        xg_words = [sb.tile([P, H], U32, name="xg_words%d" % u, align_bytes=64) for u in range(2)]
-        for u in range(2):
-            nc.vector.tensor_copy(xg_words[u][:], x_words[:].indirect(list1[:, 8 * u : 8 * u + 8]))
-            nc.vector.tensor_copy(wp_plane[:, 2 * u : 2 * u + 2, :], w8[:, 2 * u : 2 * u + 2, :])
+        xg_words = sb.tile([P, J], U32, name="xg_words", align_bytes=64)
+        nc.vector.tensor_copy(xg_words[:], x_words[:].indirect(list1[:]))
         x3_words = sb.tile([P, O], U32, name="x3_words", align_bytes=64)
         nc.vector.tensor_copy(x3_words[:], x_words[:].indirect(list3[:]))
-
-        hid = sb.tile([P, PACK, O], BF16, name="hid", align_bytes=64)
-        g1 = [sb.tile([P, J], F32, name="g1_%d" % t, align_bytes=64) for t in range(PACK)]
-        split = [[ps.tile([P, H], F32, name="a%d_%d" % (t, u)) for u in range(2)] for t in range(2)]
-        whole = [ps.tile([P, J], F32, name="a%d" % t) for t in range(2, PACK)]
-
-        def first(t, u):
-            dst = split[t][u][:] if t < 2 else whole[t - 2][:, u * H : (u + 1) * H]
-            nc.tensor.matmul_mx(
-                out=dst,
-                lhsT=wp_words[:, t, :].bitcast(E2M1),
-                lhsT_scale=wp_plane[:, t, :],
-                rhs=xg_words[u][:].bitcast(E4M3),
-                rhs_scale=xg_plane[:, u * H : (u + 1) * H],
-                start=True,
-                stop=True,
-            )
-
-        def pick(t):
-            nc.scalar.activation(hid[:, t, :], g1[t][:].indirect(list2[:]), COPY, scale=sa_t[:, t : t + 1])
-
-        for t in range(2):
-            first(t, 0)
-            nc.scalar.activation(g1[t][:, 0:H], split[t][0][:], RELU)
-        for t in range(2):
-            first(t, 1)
-            nc.vector.tensor_scalar_max(g1[t][:, H:J], split[t][1][:], 0.0)
-            pick(t)
-        for t in range(2, PACK):
-            first(t, 0)
-            first(t, 1)
-            nc.vector.tensor_scalar_max(g1[t][:], whole[t - 2][:], 0.0)
-            pick(t)
-
         x3_plane = sb.tile([P, O], U8, name="x3_plane", align_bytes=64)
         nc.vector.tensor_copy(x3_plane[:], x_plane[:].indirect(list3[:]))
 
-        nc.vector.tensor_copy(out_two[64:128, 0].bitcast(I32), out_two[0:64, 1].bitcast(I32))
+        hid = sb.tile([P, PACK, O], BF16, name="hid", align_bytes=64)
+        for t in range(PACK):
+            acc = ps.tile([P, J], F32, name="a%d" % t)
+            nc.tensor.matmul_mx(
+                out=acc[:],
+                lhsT=wp_words[:, t, :].bitcast(E2M1),
+                lhsT_scale=wp_plane[:, t, :],
+                rhs=xg_words[:].bitcast(E4M3),
+                rhs_scale=xg_plane[:],
+                start=True,
+                stop=True,
+            )
+            g1 = sb.tile([P, J], F32, name="g1_%d" % t, align_bytes=64)
+            if t == 0:
+                nc.scalar.activation(g1[:], acc[:], RELU)
+            else:
+                nc.vector.tensor_scalar_max(g1[:], acc[:], 0.0)
+            nc.scalar.activation(hid[:, t, :], g1[:].indirect(list2[:]), COPY, scale=sa_t[:, t : t + 1])
 
         ys = [ps.tile([P, O], F32, name="y%d" % h) for h in range(2)]
         for h in range(2):

@@ -32,6 +32,7 @@ def tile_list_groupshift_solo_further_plain_kernel(
 
     with ExitStack() as ctx:
         sb = ctx.enter_context(tc.tile_pool(name="sb", bufs=1))
+        shared = ctx.enter_context(tc.tile_pool(name="shared", bufs=1))
         ps = ctx.enter_context(tc.psum_pool(name="ps", bufs=1))
 
         list1 = sb.tile([P, J // 16], U16, name="list1")
@@ -40,7 +41,7 @@ def tile_list_groupshift_solo_further_plain_kernel(
         x_words = sb.tile([P, T], U32, name="x_words", align_bytes=64)
         x_plane = sb.tile([P, T], U8, name="x_plane", align_bytes=64)
         w_raw = sb.tile([P, 2 * R], U8, name="w_raw", align_bytes=64)
-        w_two = sb.tile([P, 2, R], U8, name="w_two", align_bytes=64)
+        w_two = shared.tile([P, 2, R], U8, name="w_two", align_bytes=64, offset=0)
         sa_t = sb.tile([P, PACK], F32, name="sa_t")
         ws_w = sb.tile([P, N], U32, name="ws_w", align_bytes=64)
         wb_w = sb.tile([P, N], U32, name="wb_w", align_bytes=64)
@@ -76,8 +77,6 @@ def tile_list_groupshift_solo_further_plain_kernel(
         for b in range(2):
             nc.vector.tensor_copy(w_two[32 * b : 32 * b + 4].bitcast(I32), by_parity[:, b])
         nc.vector.tensor_copy(w_two[64:128, 0, :].bitcast(I32), w_two[0:64, 1, :].bitcast(I32))
-        xg_plane = sb.tile([P, J], U8, name="xg_plane", align_bytes=64)
-        nc.vector.tensor_copy(xg_plane[:], x_plane[:].indirect(list1[:]))
         wp_plane = sb.tile([P, PACK, P], U8, name="wp_plane", align_bytes=64)
         nc.vector.tensor_copy(wp_plane[:], w_two[:, 0, :].rearrange("p (m t) -> p t m", t=PACK))
 
@@ -86,11 +85,14 @@ def tile_list_groupshift_solo_further_plain_kernel(
         for t in range(PACK):
             nc.scalar.copy(wp_words[:, t, :].bitcast(U16), w16[:, t, :])
 
-        xg_words = sb.tile([P, J], U32, name="xg_words", align_bytes=64)
-        nc.vector.tensor_copy(xg_words[:], x_words[:].indirect(list1[:]))
-        x3_words = sb.tile([P, O], U32, name="x3_words", align_bytes=64)
-        nc.vector.tensor_copy(x3_words[:], x_words[:].indirect(list3[:]))
-        x3_plane = sb.tile([P, O], U8, name="x3_plane", align_bytes=64)
+        xg_plane = shared.tile([P, J], U8, name="xg_plane", align_bytes=64, offset=0)
+        x3_plane = shared.tile([P, O], U8, name="x3_plane", align_bytes=64, offset=J)
+        picked = shared.tile([P, J + O], U32, name="picked", align_bytes=64, offset=J + O)
+        xg_words = picked[:, 0:J]
+        x3_words = picked[:, J : J + O]
+        nc.vector.tensor_copy(xg_words, x_words[:].indirect(list1[:]))
+        nc.vector.tensor_copy(xg_plane[:], x_plane[:].indirect(list1[:]))
+        nc.vector.tensor_copy(x3_words, x_words[:].indirect(list3[:]))
         nc.vector.tensor_copy(x3_plane[:], x_plane[:].indirect(list3[:]))
 
         hid = sb.tile([P, PACK, O], BF16, name="hid", align_bytes=64)

from contextlib import ExitStack

import concourse.mybir as mybir

K, T, J, R, O, N = 512, 1024, 256, 512, 128, 256
FLOPS = 2 * K * R * J + 2 * R * N * O + 2 * K * N * O

F32 = mybir.dt.float32
BF16 = mybir.dt.bfloat16
I32 = mybir.dt.int32
U32 = mybir.dt.uint32
U16 = mybir.dt.uint16
U8 = mybir.dt.uint8
E4M3 = mybir.dt.float8_e4m3fn_x4
E5M2 = mybir.dt.float8_e5m2_x4
E2M1 = mybir.dt.float4_e2m1fn_x4
COPY = mybir.ActivationFunctionType.Copy
RELU = mybir.ActivationFunctionType.Relu

P = 128
PACK = 4
QUADS = 4


def tile_list_groupshift_solo_further_plain_kernel(
    tc, xt_words, xt_scales, w_words, w_scales, sa, wb_words, wb_scales, ws_words, ws_scales, offs, offs2, offs3, out
):
    nc = tc.nc

    def words(ap):
        return ap[0].rearrange("p n t -> p (n t)").bitcast(I32)

    with ExitStack() as ctx:
        sb = ctx.enter_context(tc.tile_pool(name="sb", bufs=1))
        shared = ctx.enter_context(tc.tile_pool(name="shared", bufs=1))
        ps = ctx.enter_context(tc.psum_pool(name="ps", bufs=1))

        list1 = sb.tile([P, J // 16], U16, name="list1")
        list2 = sb.tile([P, O // 16], U16, name="list2")
        list3 = sb.tile([P, O // 16], U16, name="list3")
        x_words = sb.tile([P, T], U32, name="x_words", align_bytes=64)
        x_plane = sb.tile([P, T], U8, name="x_plane", align_bytes=64)
        w_raw = sb.tile([P, 2 * R], U8, name="w_raw", align_bytes=64)
        w_two = shared.tile([P, 2, R], U8, name="w_two", align_bytes=64, offset=0)
        sa_t = sb.tile([P, PACK], F32, name="sa_t")
        ws_w = sb.tile([P, N], U32, name="ws_w", align_bytes=64)
        wb_w = sb.tile([P, N], U32, name="wb_w", align_bytes=64)
        w_stage = sb.tile([4, QUADS, R // 4], I32, name="w_stage")
        ws_plane = sb.tile([P, N], U8, name="ws_plane", align_bytes=64)
        wb_plane = sb.tile([P, N], U8, name="wb_plane", align_bytes=64)

        def load_plane(plane, scales):
            for q in range(QUADS):
                nc.sync.dma_start(
                    plane[32 * q : 32 * q + 4, :].bitcast(I32), scales[0, 4 * q : 4 * q + 4, :].bitcast(I32)
                )

        nc.vector.memset(x_plane[:].bitcast(I32), 0)
        nc.vector.memset(w_two[0:64].bitcast(I32), 0)
        nc.vector.memset(ws_plane[:].bitcast(I32), 0)
        nc.vector.memset(wb_plane[:].bitcast(I32), 0)

        nc.sync.dma_start(list1[:], offs)
        nc.scalar.dma_start(w_stage[:], w_scales[0].bitcast(I32).rearrange("(q r) n -> r q n", r=4))
        nc.scalar.dma_start(x_words[:].bitcast(I32), words(xt_words))
        nc.sync.dma_start(w_raw[:].bitcast(I32), w_words[0].bitcast(I32))
        load_plane(x_plane, xt_scales)
        nc.gpsimd.dma_start(sa_t[:], sa.rearrange("(p t) o -> p (t o)", t=PACK))
        nc.sync.dma_start(list3[:], offs3)
        nc.sync.dma_start(list2[:], offs2)
        nc.gpsimd.dma_start(ws_w[:].bitcast(I32), words(ws_words))
        nc.gpsimd.dma_start(wb_w[:].bitcast(I32), words(wb_words))
        load_plane(ws_plane, ws_scales)
        load_plane(wb_plane, wb_scales)

        by_parity = w_stage[:].rearrange("r (a b) n -> r b a n", b=2)
        for b in range(2):
            nc.vector.tensor_copy(w_two[32 * b : 32 * b + 4].bitcast(I32), by_parity[:, b])
        nc.vector.tensor_copy(w_two[64:128, 0, :].bitcast(I32), w_two[0:64, 1, :].bitcast(I32))
        wp_plane = sb.tile([P, PACK, P], U8, name="wp_plane", align_bytes=64)
        nc.vector.tensor_copy(wp_plane[:], w_two[:, 0, :].rearrange("p (m t) -> p t m", t=PACK))

        wp_words = sb.tile([P, PACK, 2 * P], U8, name="wp_words", align_bytes=64)
        w16 = w_raw[:].bitcast(U16).rearrange("p (m t) -> p t m", t=PACK)
        for t in range(PACK):
            nc.scalar.copy(wp_words[:, t, :].bitcast(U16), w16[:, t, :])

        xg_plane = shared.tile([P, J], U8, name="xg_plane", align_bytes=64, offset=0)
        x3_plane = shared.tile([P, O], U8, name="x3_plane", align_bytes=64, offset=J)
        picked = shared.tile([P, J + O], U32, name="picked", align_bytes=64, offset=J + O)
        xg_words = picked[:, 0:J]
        x3_words = picked[:, J : J + O]
        nc.vector.tensor_copy(xg_words, x_words[:].indirect(list1[:]))
        nc.vector.tensor_copy(xg_plane[:], x_plane[:].indirect(list1[:]))
        nc.vector.tensor_copy(x3_words, x_words[:].indirect(list3[:]))
        nc.vector.tensor_copy(x3_plane[:], x_plane[:].indirect(list3[:]))

        hid = sb.tile([P, PACK, O], BF16, name="hid", align_bytes=64)
        for t in range(PACK):
            acc = ps.tile([P, J], F32, name="a%d" % t)
            nc.tensor.matmul_mx(
                out=acc[:],
                lhsT=wp_words[:, t, :].bitcast(E2M1),
                lhsT_scale=wp_plane[:, t, :],
                rhs=xg_words[:].bitcast(E4M3),
                rhs_scale=xg_plane[:],
                start=True,
                stop=True,
            )
            g1 = sb.tile([P, J], F32, name="g1_%d" % t, align_bytes=64)
            if t == 0:
                nc.scalar.activation(g1[:], acc[:], RELU)
            else:
                nc.vector.tensor_scalar_max(g1[:], acc[:], 0.0)
            nc.scalar.activation(hid[:, t, :], g1[:].indirect(list2[:]), COPY, scale=sa_t[:, t : t + 1])

        ys = [ps.tile([P, O], F32, name="y%d" % h) for h in range(2)]
        for h in range(2):
            cols = slice(h * P, (h + 1) * P)
            nc.tensor.matmul_mx(
                out=ys[h][:],
                lhsT=ws_w[:, cols].bitcast(E5M2),
                lhsT_scale=ws_plane[:, cols],
                rhs=x3_words[:].bitcast(E4M3),
                rhs_scale=x3_plane[:],
                start=True,
                stop=False,
            )

        woven = sb.tile([P, O, PACK], BF16, name="woven", align_bytes=64)
        nc.vector.tensor_copy(
            woven[:].rearrange("p (c i) t -> p c t i", i=4),
            hid[:].rearrange("p t (c i) -> p c t i", i=4),
        )
        h_words = sb.tile([P, O], U32, name="h_words", align_bytes=64)
        h_plane = sb.tile([P, O], U8, name="h_plane", align_bytes=64)
        nc.vector.quantize_mx(
            out=h_words[:].bitcast(E4M3), scales=h_plane[:], in_=woven[:].rearrange("p o t -> p (o t)")
        )

        for h in range(2):
            cols = slice(h * P, (h + 1) * P)
            nc.tensor.matmul_mx(
                out=ys[h][:],
                lhsT=wb_w[:, cols].bitcast(E5M2),
                lhsT_scale=wb_plane[:, cols],
                rhs=h_words[:].bitcast(E4M3),
                rhs_scale=h_plane[:],
                start=False,
                stop=True,
            )
        res0 = sb.tile([P, O], F32, name="res0")
        res1 = sb.tile([P, O], F32, name="res1")
        nc.vector.tensor_copy(res0[:], ys[0][:])
        nc.sync.dma_start(out[0:P, :], res0[:])
        nc.scalar.copy(res1[:], ys[1][:])
        nc.scalar.dma_start(out[P : 2 * P, :], res1[:])
